import numpy as np
import ml_dtypes


def mxq(x, axis, fmt="e4m3"):
    dtype, down = {"e4m3": (ml_dtypes.float8_e4m3fn, 7), "e5m2": (ml_dtypes.float8_e5m2, 14)}[fmt]
    v = np.moveaxis(np.asarray(x, np.float32).astype(ml_dtypes.bfloat16).astype(np.float64), axis, -1)
    blocks = v.reshape(v.shape[:-1] + (-1, 32))
    amax = np.abs(blocks).max(-1, keepdims=True)
    byte = np.maximum(np.where(amax > 0, np.frexp(amax)[1] - 1 + 127, 0) - down, 1)
    scale = np.exp2(byte - 127.0)
    codes = (blocks / scale).astype(np.float32).astype(dtype).astype(np.float64)
    return np.moveaxis((codes * scale).reshape(v.shape), -1, axis)


WIDE = False


def mx_kscale(k):
    if not WIDE:
        return np.ones(k)
    levels = np.array([30, -30])
    if k % 512:
        return np.exp2(np.random.permutation(np.resize(levels, k // 32))).repeat(32)
    a = np.empty((k // 512, 16))
    for p in range(k // 512):
        a[p, :8] = np.random.permutation(np.resize(levels, 8))
        for g in range(8):
            far = levels[np.abs(levels - a[p, g]) >= 10]
            a[p, g + 8] = far[np.random.randint(len(far))]
    return np.exp2(a.ravel()).repeat(32)


def f64(x):
    return np.asarray(x).astype(np.float64)


def striped(idx):
    return np.tile(np.asarray(idx).reshape(-1, 16).T, (8, 1)).astype(np.uint16)


def unstriped(offs):
    return offs[:16].T.reshape(-1).astype(np.int64)


E2M1 = np.array([0.0, 0.5, 1.0, 1.5, 2.0, 3.0, 4.0, 6.0, -0.0, -0.5, -1.0, -1.5, -2.0, -3.0, -4.0, -6.0])


def pack_weight(w, fmt):
    k, n = w.shape
    w = f64(np.asarray(w, np.float32).astype(ml_dtypes.bfloat16)).reshape(k // 32, 32, n)
    amax = np.abs(w).max(1)
    if fmt in ("e4m3", "e5m2"):
        byte = np.frexp(amax)[1] - 1 + 127 - (7 if fmt == "e4m3" else 14)
    else:
        mant, ex = np.frexp(amax / 6.0)
        byte = np.where(mant > 0.5, ex, ex - 1) + 127
    byte = np.clip(np.where(amax > 0, byte, 1), 1, 254)
    scaled = (w * np.exp2(127.0 - byte)[:, None, :]).reshape(k, n).astype(np.float32)
    by_word = np.ascontiguousarray(scaled.reshape(k // 512, 128, 4, n).transpose(0, 1, 3, 2))
    if fmt in ("e4m3", "e5m2"):
        words = by_word.astype(ml_dtypes.float8_e4m3fn if fmt == "e4m3" else ml_dtypes.float8_e5m2).view(np.uint8)
    else:
        c = by_word.astype(ml_dtypes.float4_e2m1fn).view(np.uint8) & 0xF
        words = (c[..., 0::2] | (c[..., 1::2] << 4)).reshape(k // 512, 128, 2 * n)
    return np.ascontiguousarray(words), np.ascontiguousarray(byte.astype(np.uint8).reshape(k // 512, 16, n))


def unpack_weight(words, scales, fmt):
    g, _, n = scales.shape
    words = np.ascontiguousarray(words).reshape(g, 128, n, -1)
    if fmt in ("e4m3", "e5m2"):
        vals = words.view(ml_dtypes.float8_e4m3fn if fmt == "e4m3" else ml_dtypes.float8_e5m2).astype(np.float64)
    else:
        nib = np.empty((g, 128, n, 4), np.uint8)
        nib[..., 0::2] = words & 0xF
        nib[..., 1::2] = words >> 4
        vals = E2M1[nib]
    vals = vals * np.repeat(np.exp2(scales.astype(np.float64) - 127.0), 8, axis=1)[..., None]
    return vals.transpose(0, 1, 3, 2).reshape(g * 512, n)


K, T, Z, J, R, C, N, E = 512, 1024, 1024, 256, 512, 512, 256, 128


def setup_inputs():
    n = np.random.standard_normal
    idx = np.random.permutation(T)[:J]
    idx2 = np.random.permutation(Z)[:J]
    idx3 = np.random.permutation(C)[:J]
    idx4 = np.random.permutation(C)[:J]
    idx5 = np.random.permutation(J)[:E]
    idx6 = np.random.permutation(J)[:E]
    fk = mx_kscale(K)
    fr = mx_kscale(R)
    xtp = pack_weight(n((K, T)) / fk[:, None], "e2m1")
    xop = pack_weight(n((K, Z)) / fk[:, None], "e5m2")
    wp = pack_weight(n((K, R)) * 1 / np.sqrt(K) * fk[:, None] * fr, "e5m2")
    w2p = pack_weight(n((K, R)) * 1 / np.sqrt(K) * fk[:, None] * fr, "e4m3")
    wbp = pack_weight(n((R, N)) * 1 / np.sqrt(R) / fr[:, None], "e4m3")
    return {
        "xt_words": xtp[0],
        "xt_scales": xtp[1],
        "xo_words": xop[0],
        "xo_scales": xop[1],
        "w_words": wp[0],
        "w_scales": wp[1],
        "w2_words": w2p[0],
        "w2_scales": w2p[1],
        "wb_words": wbp[0],
        "wb_scales": wbp[1],
        "offs": striped(idx),
        "offs2": striped(idx2),
        "offs3": striped(idx3),
        "offs4": striped(idx4),
        "offs5": striped(idx5),
        "offs6": striped(idx6),
    }


def reference(xt_words, xt_scales, xo_words, xo_scales, w_words, w_scales, w2_words, w2_scales, wb_words, wb_scales, offs, offs2, offs3, offs4, offs5, offs6):
    idx = unstriped(offs)
    idx2 = unstriped(offs2)
    idx3 = unstriped(offs3)
    idx4 = unstriped(offs4)
    idx5 = unstriped(offs5)
    idx6 = unstriped(offs6)
    xtu = unpack_weight(xt_words, xt_scales, "e2m1")
    xou = unpack_weight(xo_words, xo_scales, "e5m2")
    wu = unpack_weight(w_words, w_scales, "e5m2")
    w2u = unpack_weight(w2_words, w2_scales, "e4m3")
    wbu = unpack_weight(wb_words, wb_scales, "e4m3")
    xtidxg = xtu[:, idx]
    xoidx2g = xou[:, idx2]
    a = wu.T @ xtidxg + w2u.T @ xoidx2g
    b = w2u.T @ xtidxg + wu.T @ xoidx2g
    pw = np.zeros((R, C))
    pw[:, idx3] = a
    hid = np.abs(pw[:, idx4] - b)
    hidq = mxq(hid, 0, "e5m2")
    p = wbu.T @ hidq
    y = np.maximum(p[:, idx5], p[:, idx6])
    return y

@@ -1,0 +1,180 @@
+from contextlib import ExitStack
+
+import concourse.mybir as mybir
+
+K, T, Z, J, R, C, N, E = 512, 1024, 1024, 256, 512, 512, 256, 128
+FLOPS = 2 * (4 * K * R * J + R * N * J)
+
+F32 = mybir.dt.float32
+BF16 = mybir.dt.bfloat16
+I32 = mybir.dt.int32
+U32 = mybir.dt.uint32
+U16 = mybir.dt.uint16
+U8 = mybir.dt.uint8
+E4M3 = mybir.dt.float8_e4m3fn_x4
+E5M2 = mybir.dt.float8_e5m2_x4
+E2M1 = mybir.dt.float4_e2m1fn_x4
+ALU = mybir.AluOpType
+ACT = mybir.ActivationFunctionType
+
+P = 128
+PACK = 4
+
+
+def tile_list_crossed_board_one_bestoftwo_kernel(
+    tc, xt_words, xt_scales, xo_words, xo_scales, w_words, w_scales, w2_words, w2_scales,
+    wb_words, wb_scales, offs, offs2, offs3, offs4, offs5, offs6, out,
+):
+    nc = tc.nc
+    with ExitStack() as ctx:
+        sb = ctx.enter_context(tc.tile_pool(name="sb", bufs=1))
+        ps = ctx.enter_context(tc.psum_pool(name="ps", bufs=1))
+
+        def load_list(src, name):
+            t = sb.tile(list(src.shape), U16, name=name)
+            nc.sync.dma_start(t[:], src)
+            return t
+
+        def load_words(queue, src, dtype, width, name):
+            t = sb.tile([P, width], dtype, name=name, align_bytes=64)
+            queue.dma_start(t[:].bitcast(I32), src.bitcast(I32))
+            return t
+
+        def zero_plane(width, name):
+            t = sb.tile([P, width], U8, name=name, align_bytes=64)
+            nc.vector.memset(t[:].bitcast(I32), 0)
+            return t
+
+        def load_plane(queue, t, src):
+            for q in range(4):
+                queue.dma_start(t[32 * q : 32 * q + 4, :].bitcast(I32), src[0, 4 * q : 4 * q + 4, :].bitcast(I32))
+
+        def flat(words):
+            return words[0].rearrange("p n t -> p (n t)")
+
+        xt_s = zero_plane(T, "xt_s")
+        xo_s = zero_plane(Z, "xo_s")
+        w_s = zero_plane(R, "w_s")
+        w2_s = zero_plane(R, "w2_s")
+        wb_s = zero_plane(N, "wb_s")
+
+        o1 = load_list(offs, "o1")
+        xt_w = load_words(nc.scalar, xt_words[0], U16, T, "xt_w")
+        o2 = load_list(offs2, "o2")
+        xo_w = load_words(nc.scalar, flat(xo_words), U32, Z, "xo_w")
+        load_plane(nc.sync, xt_s, xt_scales)
+        load_plane(nc.gpsimd, w_s, w_scales)
+        load_plane(nc.sync, xo_s, xo_scales)
+        w_w = load_words(nc.sync, flat(w_words), U32, R, "w_w")
+        w2_w = load_words(nc.sync, flat(w2_words), U32, R, "w2_w")
+        load_plane(nc.sync, w2_s, w2_scales)
+        o3 = load_list(offs3, "o3")
+        o4 = load_list(offs4, "o4")
+        wb_w = load_words(nc.sync, flat(wb_words), U32, N, "wb_w")
+        load_plane(nc.sync, wb_s, wb_scales)
+        o5 = load_list(offs5, "o5")
+        o6 = load_list(offs6, "o6")
+
+        pages = []
+        for t in range(PACK):
+            page = sb.tile([P, C], F32, name="page%d" % t)
+            nc.vector.memset(page[:], 0.0)
+            pages.append(page)
+
+        def gather(window, lst, dtype, name):
+            t = sb.tile([P, J], dtype, name=name, align_bytes=64)
+            nc.vector.tensor_copy(t[:], window[:].indirect(lst[:]))
+            return t
+
+        def deal(src, dtype, name, copy):
+            t = sb.tile([P, PACK, P], dtype, name=name, align_bytes=64)
+            copy(t[:], src[:].rearrange("p (m t) -> p t m", t=PACK))
+            return t
+
+        xt_gw = gather(xt_w, o1, U16, "xt_gw")
+        xt_gs = gather(xt_s, o1, U8, "xt_gs")
+        w_dw = deal(w_w, U32, "w_dw", nc.scalar.copy)
+        w_ds = deal(w_s, U8, "w_ds", nc.vector.tensor_copy)
+        xo_gw = gather(xo_w, o2, U32, "xo_gw")
+        xo_gs = gather(xo_s, o2, U8, "xo_gs")
+        w2_dw = deal(w2_w, U32, "w2_dw", nc.scalar.copy)
+        w2_ds = deal(w2_s, U8, "w2_ds", nc.vector.tensor_copy)
+
+        xt_op = (xt_gw[:].bitcast(E2M1), xt_gs[:])
+        xo_op = (xo_gw[:].bitcast(E5M2), xo_gs[:])
+
+        def w_op(t):
+            return (w_dw[:, t, :].bitcast(E5M2), w_ds[:, t, :])
+
+        def w2_op(t):
+            return (w2_dw[:, t, :].bitcast(E4M3), w2_ds[:, t, :])
+
+        def product(acc, lhs, rhs, start, stop):
+            nc.tensor.matmul_mx(out=acc, lhsT=lhs[0], lhsT_scale=lhs[1], rhs=rhs[0], rhs_scale=rhs[1], start=start, stop=stop)
+
+        a_ps = []
+        for t in range(PACK):
+            acc = ps.tile([P, J], F32, name="a%d" % t, tag="bank%d" % t)
+            product(acc[:], w_op(t), xt_op, True, False)
+            product(acc[:], w2_op(t), xo_op, False, True)
+            a_ps.append(acc)
+        b_ps = []
+        for t in range(PACK):
+            acc = ps.tile([P, J], F32, name="b%d" % t, tag="bank%d" % (PACK + t))
+            product(acc[:], w2_op(t), xt_op, True, False)
+            product(acc[:], w_op(t), xo_op, False, True)
+            b_ps.append(acc)
+
+        def s_copy(dst, src):
+            nc.scalar.activation(dst, src, ACT.Copy)
+
+        def v_copy(dst, src):
+            nc.vector.tensor_copy(dst, src)
+
+        diff = sb.tile([P, PACK, J], F32, name="diff")
+        a_sb = [sb.tile([P, J], F32, name="a_sb%d" % t) for t in range(PACK)]
+        got = [sb.tile([P, J], F32, name="got%d" % t) for t in range(PACK)]
+        s_copy(a_sb[0][:], a_ps[0][:])
+        v_copy(a_sb[1][:], a_ps[1][:])
+        s_copy(pages[0][:].indirect(o3[:]), a_sb[0][:])
+        v_copy(pages[1][:].indirect(o3[:]), a_sb[1][:])
+        s_copy(a_sb[2][:], a_ps[2][:])
+        s_copy(a_sb[3][:], a_ps[3][:])
+        s_copy(got[0][:], pages[0][:].indirect(o4[:]))
+        v_copy(pages[3][:].indirect(o3[:]), a_sb[3][:])
+        s_copy(pages[2][:].indirect(o3[:]), a_sb[2][:])
+        v_copy(got[1][:], pages[1][:].indirect(o4[:]))
+        s_copy(got[2][:], pages[2][:].indirect(o4[:]))
+        v_copy(got[3][:], pages[3][:].indirect(o4[:]))
+        for t in range(PACK):
+            nc.vector.tensor_tensor(diff[:, t, :], got[t][:], b_ps[t][:], ALU.subtract)
+
+        hid = sb.tile([P, J, PACK], BF16, name="hid", align_bytes=64)
+        H = J // 2
+        lo = diff[:, :, 0:H].rearrange("p t j -> p j t")
+        hi = diff[:, :, H:J].rearrange("p t j -> p j t")
+        nc.scalar.activation(hid[:, 0:H, :], lo, ACT.Abs)
+        nc.vector.scalar_tensor_tensor(hid[:, H:J, :], hi, -1.0, hi, ALU.mult, ALU.max)
+
+        h_w = sb.tile([P, J], U32, name="h_w", align_bytes=64)
+        h_s = sb.tile([P, J], U8, name="h_s", align_bytes=64)
+        nc.vector.quantize_mx(out=h_w[:].bitcast(E5M2), scales=h_s[:], in_=hid[:].rearrange("p j t -> p (j t)"))
+
+        copies = [s_copy, v_copy]
+        queues = [nc.scalar, nc.sync]
+        picked = []
+        for h in range(N // P):
+            acc = ps.tile([P, J], F32, name="p%d" % h, tag="bank%d" % h)
+            cols = slice(h * P, (h + 1) * P)
+            product(acc[:], (wb_w[:, cols].bitcast(E4M3), wb_s[:, cols]), (h_w[:].bitcast(E5M2), h_s[:]), True, True)
+            p_sb = sb.tile([P, J], F32, name="p_sb%d" % h)
+            copies[h](p_sb[:], acc[:])
+            one = sb.tile([P, E], F32, name="one%d" % h)
+            two = sb.tile([P, E], F32, name="two%d" % h)
+            copies[h](one[:], p_sb[:].indirect(o5[:]))
+            copies[h](two[:], p_sb[:].indirect(o6[:]))
+            picked.append((one, two))
+        for h in (1, 0):
+            best = sb.tile([P, E], F32, name="best%d" % h)
+            nc.vector.tensor_tensor(best[:], picked[h][0][:], picked[h][1][:], ALU.max)
+            queues[h].dma_start(out[h * P : (h + 1) * P, :], best[:])

@@ -40,34 +40,43 @@ def tile_list_crossed_board_one_bestoftwo_kernel(
             queue.dma_start(t[:].bitcast(I32), src.bitcast(I32))
             return t
 
-        def zero_plane(width, name):
+        def new_plane(engine, width, name):
             t = sb.tile([P, width], U8, name=name, align_bytes=64)
-            nc.vector.memset(t[:].bitcast(I32), 0)
+            engine.memset(t[:].bitcast(I32), 0)
             return t
+
+        def load_low(queue, t, src):
+            rows = src[0, 0:14, :].bitcast(I32).partition_broadcast(5)
+            queue.dma_start(t[0:70, :].bitcast(I32), rows)
+
+        def load_quadrant(queue, t, src, q):
+            queue.dma_start(t[32 * q : 32 * q + 4, :].bitcast(I32), src[0, 4 * q : 4 * q + 4, :].bitcast(I32))
 
         def load_plane(queue, t, src):
             for q in range(4):
-                queue.dma_start(t[32 * q : 32 * q + 4, :].bitcast(I32), src[0, 4 * q : 4 * q + 4, :].bitcast(I32))
+                load_quadrant(queue, t, src, q)
 
         def flat(words):
             return words[0].rearrange("p n t -> p (n t)")
 
-        xt_s = zero_plane(T, "xt_s")
-        xo_s = zero_plane(Z, "xo_s")
-        w_s = zero_plane(R, "w_s")
-        w2_s = zero_plane(R, "w2_s")
-        wb_s = zero_plane(N, "wb_s")
+        xt_s = new_plane(nc.vector, T, "xt_s")
+        xo_s = new_plane(nc.vector, Z, "xo_s")
+        w_s = new_plane(nc.gpsimd, R, "w_s")
+        w2_s = new_plane(nc.gpsimd, R, "w2_s")
+        wb_s = new_plane(nc.vector, N, "wb_s")
 
+        load_low(nc.gpsimd, w_s, w_scales)
+        load_low(nc.gpsimd, w2_s, w2_scales)
+        load_quadrant(nc.gpsimd, w2_s, w2_scales, 3)
         o1 = load_list(offs, "o1")
-        xt_w = load_words(nc.scalar, xt_words[0], U16, T, "xt_w")
         o2 = load_list(offs2, "o2")
-        xo_w = load_words(nc.scalar, flat(xo_words), U32, Z, "xo_w")
         load_plane(nc.sync, xt_s, xt_scales)
-        load_plane(nc.gpsimd, w_s, w_scales)
+        xt_w = load_words(nc.sync, xt_words[0], U16, T, "xt_w")
+        xo_w = load_words(nc.sync, flat(xo_words), U32, Z, "xo_w")
         load_plane(nc.sync, xo_s, xo_scales)
         w_w = load_words(nc.sync, flat(w_words), U32, R, "w_w")
         w2_w = load_words(nc.sync, flat(w2_words), U32, R, "w2_w")
-        load_plane(nc.sync, w2_s, w2_scales)
+        load_quadrant(nc.sync, w_s, w_scales, 3)
         o3 = load_list(offs3, "o3")
         o4 = load_list(offs4, "o4")
         wb_w = load_words(nc.sync, flat(wb_words), U32, N, "wb_w")
@@ -78,7 +87,8 @@ def tile_list_crossed_board_one_bestoftwo_kernel(
         pages = []
         for t in range(PACK):
             page = sb.tile([P, C], F32, name="page%d" % t)
-            nc.vector.memset(page[:], 0.0)
+            nc.vector.memset(page[:, 0 : C // 2 + 1], 0.0)
+            nc.vector.memset(page[:, C // 2 + 1 : C], 0.0)
             pages.append(page)
 
         def gather(window, lst, dtype, name):
@@ -91,13 +101,13 @@ def tile_list_crossed_board_one_bestoftwo_kernel(
             copy(t[:], src[:].rearrange("p (m t) -> p t m", t=PACK))
             return t
 
-        xt_gw = gather(xt_w, o1, U16, "xt_gw")
         xt_gs = gather(xt_s, o1, U8, "xt_gs")
-        w_dw = deal(w_w, U32, "w_dw", nc.scalar.copy)
-        w_ds = deal(w_s, U8, "w_ds", nc.vector.tensor_copy)
-        xo_gw = gather(xo_w, o2, U32, "xo_gw")
+        xt_gw = gather(xt_w, o1, U16, "xt_gw")
         xo_gs = gather(xo_s, o2, U8, "xo_gs")
+        xo_gw = gather(xo_w, o2, U32, "xo_gw")
+        w_dw = deal(w_w, U32, "w_dw", nc.scalar.copy)
         w2_dw = deal(w2_w, U32, "w2_dw", nc.scalar.copy)
+        w_ds = deal(w_s, U8, "w_ds", nc.vector.tensor_copy)
         w2_ds = deal(w2_s, U8, "w2_ds", nc.vector.tensor_copy)
 
         xt_op = (xt_gw[:].bitcast(E2M1), xt_gs[:])
@@ -112,18 +122,14 @@ def tile_list_crossed_board_one_bestoftwo_kernel(
         def product(acc, lhs, rhs, start, stop):
             nc.tensor.matmul_mx(out=acc, lhsT=lhs[0], lhsT_scale=lhs[1], rhs=rhs[0], rhs_scale=rhs[1], start=start, stop=stop)
 
-        a_ps = []
-        for t in range(PACK):
-            acc = ps.tile([P, J], F32, name="a%d" % t, tag="bank%d" % t)
-            product(acc[:], w_op(t), xt_op, True, False)
-            product(acc[:], w2_op(t), xo_op, False, True)
-            a_ps.append(acc)
-        b_ps = []
-        for t in range(PACK):
-            acc = ps.tile([P, J], F32, name="b%d" % t, tag="bank%d" % (PACK + t))
-            product(acc[:], w2_op(t), xt_op, True, False)
-            product(acc[:], w_op(t), xo_op, False, True)
-            b_ps.append(acc)
+        def two_products(name, first, second, t):
+            acc = ps.tile([P, J], F32, name="%s%d" % (name, t), tag="%s%d" % (name, t))
+            product(acc[:], first(t), xt_op, True, False)
+            product(acc[:], second(t), xo_op, False, True)
+            return acc
+
+        a_ps = [two_products("a", w_op, w2_op, t) for t in range(PACK)]
+        b_ps = [two_products("b", w2_op, w_op, t) for t in range(PACK)]
 
         def s_copy(dst, src):
             nc.scalar.activation(dst, src, ACT.Copy)
@@ -132,22 +138,15 @@ def tile_list_crossed_board_one_bestoftwo_kernel(
             nc.vector.tensor_copy(dst, src)
 
         diff = sb.tile([P, PACK, J], F32, name="diff")
-        a_sb = [sb.tile([P, J], F32, name="a_sb%d" % t) for t in range(PACK)]
-        got = [sb.tile([P, J], F32, name="got%d" % t) for t in range(PACK)]
-        s_copy(a_sb[0][:], a_ps[0][:])
-        v_copy(a_sb[1][:], a_ps[1][:])
-        s_copy(pages[0][:].indirect(o3[:]), a_sb[0][:])
-        v_copy(pages[1][:].indirect(o3[:]), a_sb[1][:])
-        s_copy(a_sb[2][:], a_ps[2][:])
-        s_copy(a_sb[3][:], a_ps[3][:])
-        s_copy(got[0][:], pages[0][:].indirect(o4[:]))
-        v_copy(pages[3][:].indirect(o3[:]), a_sb[3][:])
-        s_copy(pages[2][:].indirect(o3[:]), a_sb[2][:])
-        v_copy(got[1][:], pages[1][:].indirect(o4[:]))
-        s_copy(got[2][:], pages[2][:].indirect(o4[:]))
-        v_copy(got[3][:], pages[3][:].indirect(o4[:]))
+        movers = [v_copy, s_copy]
         for t in range(PACK):
-            nc.vector.tensor_tensor(diff[:, t, :], got[t][:], b_ps[t][:], ALU.subtract)
+            a_sb = sb.tile([P, J], F32, name="a_sb%d" % t)
+            movers[t % 2](a_sb[:], a_ps[t][:])
+            movers[t % 2](pages[t][:].indirect(o3[:]), a_sb[:])
+        for t in range(PACK):
+            read = sb.tile([P, J], F32, name="got%d" % t)
+            movers[t % 2](read[:], pages[t][:].indirect(o4[:]))
+            nc.vector.tensor_tensor(diff[:, t, :], read[:], b_ps[t][:], ALU.subtract)
 
         hid = sb.tile([P, J, PACK], BF16, name="hid", align_bytes=64)
         H = J // 2
@@ -160,11 +159,11 @@ def tile_list_crossed_board_one_bestoftwo_kernel(
         h_s = sb.tile([P, J], U8, name="h_s", align_bytes=64)
         nc.vector.quantize_mx(out=h_w[:].bitcast(E5M2), scales=h_s[:], in_=hid[:].rearrange("p j t -> p (j t)"))
 
-        copies = [s_copy, v_copy]
-        queues = [nc.scalar, nc.sync]
+        copies = [v_copy, s_copy]
+        queues = [nc.sync, nc.scalar]
         picked = []
         for h in range(N // P):
-            acc = ps.tile([P, J], F32, name="p%d" % h, tag="bank%d" % h)
+            acc = ps.tile([P, J], F32, name="p%d" % h, tag="a%d" % h)
             cols = slice(h * P, (h + 1) * P)
             product(acc[:], (wb_w[:, cols].bitcast(E4M3), wb_s[:, cols]), (h_w[:].bitcast(E5M2), h_s[:]), True, True)
             p_sb = sb.tile([P, J], F32, name="p_sb%d" % h)
@@ -174,7 +173,7 @@ def tile_list_crossed_board_one_bestoftwo_kernel(
             copies[h](one[:], p_sb[:].indirect(o5[:]))
             copies[h](two[:], p_sb[:].indirect(o6[:]))
             picked.append((one, two))
-        for h in (1, 0):
+        for h in range(N // P):
             best = sb.tile([P, E], F32, name="best%d" % h)
             nc.vector.tensor_tensor(best[:], picked[h][0][:], picked[h][1][:], ALU.max)
             queues[h].dma_start(out[h * P : (h + 1) * P, :], best[:])

@@ -45,10 +45,6 @@ def tile_list_crossed_board_one_bestoftwo_kernel(
             engine.memset(t[:].bitcast(I32), 0)
             return t
 
-        def load_low(queue, t, src):
-            rows = src[0, 0:14, :].bitcast(I32).partition_broadcast(5)
-            queue.dma_start(t[0:70, :].bitcast(I32), rows)
-
         def load_quadrant(queue, t, src, q):
             queue.dma_start(t[32 * q : 32 * q + 4, :].bitcast(I32), src[0, 4 * q : 4 * q + 4, :].bitcast(I32))
 
@@ -60,23 +56,23 @@ def tile_list_crossed_board_one_bestoftwo_kernel(
             return words[0].rearrange("p n t -> p (n t)")
 
         xt_s = new_plane(nc.vector, T, "xt_s")
+        w_s = new_plane(nc.vector, R, "w_s")
         xo_s = new_plane(nc.vector, Z, "xo_s")
-        w_s = new_plane(nc.gpsimd, R, "w_s")
-        w2_s = new_plane(nc.gpsimd, R, "w2_s")
+        w2_s = new_plane(nc.vector, R, "w2_s")
         wb_s = new_plane(nc.vector, N, "wb_s")
 
-        load_low(nc.gpsimd, w_s, w_scales)
-        load_low(nc.gpsimd, w2_s, w2_scales)
-        load_quadrant(nc.gpsimd, w2_s, w2_scales, 3)
         o1 = load_list(offs, "o1")
         o2 = load_list(offs2, "o2")
         load_plane(nc.sync, xt_s, xt_scales)
         xt_w = load_words(nc.sync, xt_words[0], U16, T, "xt_w")
         xo_w = load_words(nc.sync, flat(xo_words), U32, Z, "xo_w")
-        load_plane(nc.sync, xo_s, xo_scales)
+        load_plane(nc.sync, w_s, w_scales)
+        load_quadrant(nc.sync, xo_s, xo_scales, 0)
         w_w = load_words(nc.sync, flat(w_words), U32, R, "w_w")
         w2_w = load_words(nc.sync, flat(w2_words), U32, R, "w2_w")
-        load_quadrant(nc.sync, w_s, w_scales, 3)
+        for q in range(1, 4):
+            load_quadrant(nc.sync, xo_s, xo_scales, q)
+        load_plane(nc.sync, w2_s, w2_scales)
         o3 = load_list(offs3, "o3")
         o4 = load_list(offs4, "o4")
         wb_w = load_words(nc.sync, flat(wb_words), U32, N, "wb_w")
@@ -87,8 +83,7 @@ def tile_list_crossed_board_one_bestoftwo_kernel(
         pages = []
         for t in range(PACK):
             page = sb.tile([P, C], F32, name="page%d" % t)
-            nc.vector.memset(page[:, 0 : C // 2 + 1], 0.0)
-            nc.vector.memset(page[:, C // 2 + 1 : C], 0.0)
+            nc.vector.memset(page[:], 0.0)
             pages.append(page)
 
         def gather(window, lst, dtype, name):
@@ -103,11 +98,11 @@ def tile_list_crossed_board_one_bestoftwo_kernel(
 
         xt_gs = gather(xt_s, o1, U8, "xt_gs")
         xt_gw = gather(xt_w, o1, U16, "xt_gw")
-        xo_gs = gather(xo_s, o2, U8, "xo_gs")
         xo_gw = gather(xo_w, o2, U32, "xo_gw")
+        w_ds = deal(w_s, U8, "w_ds", nc.vector.tensor_copy)
         w_dw = deal(w_w, U32, "w_dw", nc.scalar.copy)
         w2_dw = deal(w2_w, U32, "w2_dw", nc.scalar.copy)
-        w_ds = deal(w_s, U8, "w_ds", nc.vector.tensor_copy)
+        xo_gs = gather(xo_s, o2, U8, "xo_gs")
         w2_ds = deal(w2_s, U8, "w2_ds", nc.vector.tensor_copy)
 
         xt_op = (xt_gw[:].bitcast(E2M1), xt_gs[:])
@@ -143,29 +138,44 @@ def tile_list_crossed_board_one_bestoftwo_kernel(
             a_sb = sb.tile([P, J], F32, name="a_sb%d" % t)
             movers[t % 2](a_sb[:], a_ps[t][:])
             movers[t % 2](pages[t][:].indirect(o3[:]), a_sb[:])
-        for t in range(PACK):
-            read = sb.tile([P, J], F32, name="got%d" % t)
-            movers[t % 2](read[:], pages[t][:].indirect(o4[:]))
-            nc.vector.tensor_tensor(diff[:, t, :], read[:], b_ps[t][:], ALU.subtract)
-
-        hid = sb.tile([P, J, PACK], BF16, name="hid", align_bytes=64)
         H = J // 2
-        lo = diff[:, :, 0:H].rearrange("p t j -> p j t")
-        hi = diff[:, :, H:J].rearrange("p t j -> p j t")
-        nc.scalar.activation(hid[:, 0:H, :], lo, ACT.Abs)
-        nc.vector.scalar_tensor_tensor(hid[:, H:J, :], hi, -1.0, hi, ALU.mult, ALU.max)
+        halves = [slice(0, H), slice(H, J)]
+        list_halves = [slice(0, H // 16), slice(H // 16, J // 16)]
+        read = [sb.tile([P, J], F32, name="read%d" % t) for t in range(PACK)]
+        for t in range(2):
+            movers[t](read[t][:], pages[t][:].indirect(o4[:]))
+            nc.vector.tensor_tensor(diff[:, t, :], read[t][:], b_ps[t][:], ALU.subtract)
+        for h in range(2):
+            for t in range(2, PACK):
+                movers[t % 2](read[t][:, halves[h]], pages[t][:].indirect(o4[:, list_halves[h]]))
+        for h in range(2):
+            for t in range(2, PACK):
+                nc.vector.tensor_tensor(diff[:, t, halves[h]], read[t][:, halves[h]], b_ps[t][:, halves[h]], ALU.subtract)
 
-        h_w = sb.tile([P, J], U32, name="h_w", align_bytes=64)
-        h_s = sb.tile([P, J], U8, name="h_s", align_bytes=64)
-        nc.vector.quantize_mx(out=h_w[:].bitcast(E5M2), scales=h_s[:], in_=hid[:].rearrange("p j t -> p (j t)"))
+        hid_ops = []
+        for h in range(2):
+            hid = sb.tile([P, H, PACK], BF16, name="hid%d" % h, align_bytes=64)
+            part = diff[:, :, halves[h]].rearrange("p t j -> p j t")
+            if h == 0:
+                nc.scalar.activation(hid[:], part, ACT.Abs)
+            else:
+                nc.vector.scalar_tensor_tensor(hid[:], part, -1.0, part, ALU.mult, ALU.max)
+            h_w = sb.tile([P, H], U32, name="h_w%d" % h, align_bytes=64)
+            h_s = sb.tile([P, H], U8, name="h_s%d" % h, align_bytes=64)
+            hid_ops.append((hid, h_w, h_s))
+        p_ps = [ps.tile([P, J], F32, name="p%d" % n, tag="a%d" % n) for n in range(N // P)]
+        for h in range(2):
+            hid, h_w, h_s = hid_ops[h]
+            nc.vector.quantize_mx(out=h_w[:].bitcast(E5M2), scales=h_s[:], in_=hid[:].rearrange("p j t -> p (j t)"))
+            for n in range(N // P):
+                cols = slice(n * P, (n + 1) * P)
+                product(p_ps[n][:, halves[h]], (wb_w[:, cols].bitcast(E4M3), wb_s[:, cols]), (h_w[:].bitcast(E5M2), h_s[:]), True, True)
 
         copies = [v_copy, s_copy]
         queues = [nc.sync, nc.scalar]
         picked = []
         for h in range(N // P):
-            acc = ps.tile([P, J], F32, name="p%d" % h, tag="a%d" % h)
-            cols = slice(h * P, (h + 1) * P)
-            product(acc[:], (wb_w[:, cols].bitcast(E4M3), wb_s[:, cols]), (h_w[:].bitcast(E5M2), h_s[:]), True, True)
+            acc = p_ps[h]
             p_sb = sb.tile([P, J], F32, name="p_sb%d" % h)
             copies[h](p_sb[:], acc[:])
             one = sb.tile([P, E], F32, name="one%d" % h)

@@ -19,6 +19,10 @@ ACT = mybir.ActivationFunctionType
 
 P = 128
 PACK = 4
+QUADRANTS = 4
+LIST_ROWS = 16
+HALF = J // 2
+SHARE = HALF // 2
 
 
 def tile_list_crossed_board_one_bestoftwo_kernel(
@@ -31,159 +35,169 @@ def tile_list_crossed_board_one_bestoftwo_kernel(
         ps = ctx.enter_context(tc.psum_pool(name="ps", bufs=1))
 
         def load_list(src, name):
-            t = sb.tile(list(src.shape), U16, name=name)
-            nc.sync.dma_start(t[:], src)
-            return t
+            lst = sb.tile(list(src.shape), U16, name=name)
+            nc.sync.dma_start(lst[:], src)
+            return lst
 
-        def load_words(queue, src, dtype, width, name):
-            t = sb.tile([P, width], dtype, name=name, align_bytes=64)
-            queue.dma_start(t[:].bitcast(I32), src.bitcast(I32))
-            return t
+        def load_words(src, dtype, width, name):
+            words = sb.tile([P, width], dtype, name=name, align_bytes=64)
+            nc.sync.dma_start(words[:].bitcast(I32), src.bitcast(I32))
+            return words
 
-        def new_plane(engine, width, name):
-            t = sb.tile([P, width], U8, name=name, align_bytes=64)
-            engine.memset(t[:].bitcast(I32), 0)
-            return t
+        def zeroed_plane(width, name):
+            plane = sb.tile([P, width], U8, name=name, align_bytes=64)
+            nc.vector.memset(plane[:].bitcast(I32), 0)
+            return plane
 
-        def load_quadrant(queue, t, src, q):
-            queue.dma_start(t[32 * q : 32 * q + 4, :].bitcast(I32), src[0, 4 * q : 4 * q + 4, :].bitcast(I32))
-
-        def load_plane(queue, t, src):
-            for q in range(4):
-                load_quadrant(queue, t, src, q)
+        def load_scales(plane, src, quadrants):
+            for q in quadrants:
+                nc.sync.dma_start(
+                    plane[32 * q : 32 * q + 4, :].bitcast(I32), src[0, 4 * q : 4 * q + 4, :].bitcast(I32)
+                )
 
         def flat(words):
             return words[0].rearrange("p n t -> p (n t)")
 
-        xt_s = new_plane(nc.vector, T, "xt_s")
-        w_s = new_plane(nc.vector, R, "w_s")
-        xo_s = new_plane(nc.vector, Z, "xo_s")
-        w2_s = new_plane(nc.vector, R, "w2_s")
-        wb_s = new_plane(nc.vector, N, "wb_s")
+        xt_plane = zeroed_plane(T, "xt_plane")
+        w_plane = zeroed_plane(R, "w_plane")
+        xo_plane = zeroed_plane(Z, "xo_plane")
+        w2_plane = zeroed_plane(R, "w2_plane")
+        wb_plane = zeroed_plane(N, "wb_plane")
 
-        o1 = load_list(offs, "o1")
-        o2 = load_list(offs2, "o2")
-        load_plane(nc.sync, xt_s, xt_scales)
-        xt_w = load_words(nc.sync, xt_words[0], U16, T, "xt_w")
-        xo_w = load_words(nc.sync, flat(xo_words), U32, Z, "xo_w")
-        load_plane(nc.sync, w_s, w_scales)
-        load_quadrant(nc.sync, xo_s, xo_scales, 0)
-        w_w = load_words(nc.sync, flat(w_words), U32, R, "w_w")
-        w2_w = load_words(nc.sync, flat(w2_words), U32, R, "w2_w")
-        for q in range(1, 4):
-            load_quadrant(nc.sync, xo_s, xo_scales, q)
-        load_plane(nc.sync, w2_s, w2_scales)
-        o3 = load_list(offs3, "o3")
-        o4 = load_list(offs4, "o4")
-        wb_w = load_words(nc.sync, flat(wb_words), U32, N, "wb_w")
-        load_plane(nc.sync, wb_s, wb_scales)
-        o5 = load_list(offs5, "o5")
-        o6 = load_list(offs6, "o6")
+        list1 = load_list(offs, "list1")
+        list2 = load_list(offs2, "list2")
+        load_scales(xt_plane, xt_scales, range(QUADRANTS))
+        xt_tab = load_words(xt_words[0], U16, T, "xt_tab")
+        xo_tab = load_words(flat(xo_words), U32, Z, "xo_tab")
+        load_scales(w_plane, w_scales, range(QUADRANTS))
+        load_scales(xo_plane, xo_scales, range(1))
+        w_raw = load_words(flat(w_words), U32, R, "w_raw")
+        w2_raw = load_words(flat(w2_words), U32, R, "w2_raw")
+        load_scales(xo_plane, xo_scales, range(1, QUADRANTS))
+        load_scales(w2_plane, w2_scales, range(QUADRANTS))
+        list3 = load_list(offs3, "list3")
+        list4 = load_list(offs4, "list4")
+        wb_codes = load_words(flat(wb_words), U32, N, "wb_codes")
+        load_scales(wb_plane, wb_scales, range(QUADRANTS))
+        list5 = load_list(offs5, "list5")
+        list6 = load_list(offs6, "list6")
 
-        pages = []
+        boards = []
         for t in range(PACK):
-            page = sb.tile([P, C], F32, name="page%d" % t)
-            nc.vector.memset(page[:], 0.0)
-            pages.append(page)
+            board = sb.tile([P, C], F32, name="board%d" % t)
+            nc.vector.memset(board[:], 0.0)
+            boards.append(board)
 
-        def gather(window, lst, dtype, name):
-            t = sb.tile([P, J], dtype, name=name, align_bytes=64)
-            nc.vector.tensor_copy(t[:], window[:].indirect(lst[:]))
-            return t
+        def gather_packed(window, lst, dtype, name):
+            picked = sb.tile([P, J], dtype, name=name, align_bytes=64)
+            nc.vector.tensor_copy(picked[:], window[:].indirect(lst[:]))
+            return picked
 
-        def deal(src, dtype, name, copy):
-            t = sb.tile([P, PACK, P], dtype, name=name, align_bytes=64)
-            copy(t[:], src[:].rearrange("p (m t) -> p t m", t=PACK))
-            return t
+        def deal(src, dtype, name, copy, parts):
+            dealt = sb.tile([P, PACK, P], dtype, name=name, align_bytes=64)
+            by_slice = src[:].rearrange("p (m t) -> p t m", t=PACK)
+            step = PACK // parts
+            for t in range(0, PACK, step):
+                copy(dealt[:, t : t + step, :], by_slice[:, t : t + step, :])
+            return dealt
 
-        xt_gs = gather(xt_s, o1, U8, "xt_gs")
-        xt_gw = gather(xt_w, o1, U16, "xt_gw")
-        xo_gw = gather(xo_w, o2, U32, "xo_gw")
-        w_ds = deal(w_s, U8, "w_ds", nc.vector.tensor_copy)
-        w_dw = deal(w_w, U32, "w_dw", nc.scalar.copy)
-        w2_dw = deal(w2_w, U32, "w2_dw", nc.scalar.copy)
-        xo_gs = gather(xo_s, o2, U8, "xo_gs")
-        w2_ds = deal(w2_s, U8, "w2_ds", nc.vector.tensor_copy)
+        xt_sc = gather_packed(xt_plane, list1, U8, "xt_sc")
+        xt_codes = gather_packed(xt_tab, list1, U16, "xt_codes")
+        xo_codes = gather_packed(xo_tab, list2, U32, "xo_codes")
+        w_sc = deal(w_plane, U8, "w_sc", nc.vector.tensor_copy, 1)
+        w_codes = deal(w_raw, U32, "w_codes", nc.scalar.copy, 1)
+        w2_codes = deal(w2_raw, U32, "w2_codes", nc.scalar.copy, 1)
+        xo_sc = gather_packed(xo_plane, list2, U8, "xo_sc")
+        w2_sc = deal(w2_plane, U8, "w2_sc", nc.vector.tensor_copy, 2)
 
-        xt_op = (xt_gw[:].bitcast(E2M1), xt_gs[:])
-        xo_op = (xo_gw[:].bitcast(E5M2), xo_gs[:])
+        def xt_op(cols):
+            return (xt_codes[:, cols].bitcast(E2M1), xt_sc[:, cols])
+
+        def xo_op(cols):
+            return (xo_codes[:, cols].bitcast(E5M2), xo_sc[:, cols])
 
         def w_op(t):
-            return (w_dw[:, t, :].bitcast(E5M2), w_ds[:, t, :])
+            return (w_codes[:, t, :].bitcast(E5M2), w_sc[:, t, :])
 
         def w2_op(t):
-            return (w2_dw[:, t, :].bitcast(E4M3), w2_ds[:, t, :])
+            return (w2_codes[:, t, :].bitcast(E4M3), w2_sc[:, t, :])
 
         def product(acc, lhs, rhs, start, stop):
-            nc.tensor.matmul_mx(out=acc, lhsT=lhs[0], lhsT_scale=lhs[1], rhs=rhs[0], rhs_scale=rhs[1], start=start, stop=stop)
+            nc.tensor.matmul_mx(
+                out=acc, lhsT=lhs[0], lhsT_scale=lhs[1], rhs=rhs[0], rhs_scale=rhs[1], start=start, stop=stop
+            )
 
-        def two_products(name, first, second, t):
-            acc = ps.tile([P, J], F32, name="%s%d" % (name, t), tag="%s%d" % (name, t))
-            product(acc[:], first(t), xt_op, True, False)
-            product(acc[:], second(t), xo_op, False, True)
-            return acc
+        all_slots = slice(0, J)
+        halves = [slice(0, HALF), slice(HALF, J)]
+        list_halves = [slice(0, HALF // LIST_ROWS), slice(HALF // LIST_ROWS, J // LIST_ROWS)]
 
-        a_ps = [two_products("a", w_op, w2_op, t) for t in range(PACK)]
-        b_ps = [two_products("b", w2_op, w_op, t) for t in range(PACK)]
+        a_acc = []
+        for t in range(PACK):
+            acc = ps.tile([P, J], F32, name="a%d" % t, tag="bank%d" % t)
+            product(acc[:], w_op(t), xt_op(all_slots), True, False)
+            product(acc[:], w2_op(t), xo_op(all_slots), False, True)
+            a_acc.append(acc)
+        b_acc = []
+        for h in range(2):
+            acc = ps.tile([P, PACK, HALF], F32, name="b%d" % h)
+            for t in range(PACK):
+                product(acc[:, t, :], w2_op(t), xt_op(halves[h]), True, False)
+                product(acc[:, t, :], w_op(t), xo_op(halves[h]), False, True)
+            b_acc.append(acc)
 
-        def s_copy(dst, src):
+        def scalar_move(dst, src):
             nc.scalar.activation(dst, src, ACT.Copy)
 
-        def v_copy(dst, src):
-            nc.vector.tensor_copy(dst, src)
+        movers = [nc.vector.tensor_copy, scalar_move]
 
-        diff = sb.tile([P, PACK, J], F32, name="diff")
-        movers = [v_copy, s_copy]
+        a_sb = [sb.tile([P, J], F32, name="a_sb%d" % t) for t in range(PACK)]
         for t in range(PACK):
-            a_sb = sb.tile([P, J], F32, name="a_sb%d" % t)
-            movers[t % 2](a_sb[:], a_ps[t][:])
-            movers[t % 2](pages[t][:].indirect(o3[:]), a_sb[:])
-        H = J // 2
-        halves = [slice(0, H), slice(H, J)]
-        list_halves = [slice(0, H // 16), slice(H // 16, J // 16)]
-        read = [sb.tile([P, J], F32, name="read%d" % t) for t in range(PACK)]
-        for t in range(2):
-            movers[t](read[t][:], pages[t][:].indirect(o4[:]))
-            nc.vector.tensor_tensor(diff[:, t, :], read[t][:], b_ps[t][:], ALU.subtract)
-        for h in range(2):
-            for t in range(2, PACK):
-                movers[t % 2](read[t][:, halves[h]], pages[t][:].indirect(o4[:, list_halves[h]]))
-        for h in range(2):
-            for t in range(2, PACK):
-                nc.vector.tensor_tensor(diff[:, t, halves[h]], read[t][:, halves[h]], b_ps[t][:, halves[h]], ALU.subtract)
+            movers[t // 2](a_sb[t][:], a_acc[t][:])
+        for t in range(PACK):
+            movers[t // 2](boards[t][:].indirect(list3[:]), a_sb[t][:])
 
-        hid_ops = []
+        read = [[sb.tile([P, 2, HALF], F32, name="read%d_%d" % (h, g)) for g in range(2)] for h in range(2)]
         for h in range(2):
-            hid = sb.tile([P, H, PACK], BF16, name="hid%d" % h, align_bytes=64)
-            part = diff[:, :, halves[h]].rearrange("p t j -> p j t")
-            if h == 0:
-                nc.scalar.activation(hid[:], part, ACT.Abs)
-            else:
-                nc.vector.scalar_tensor_tensor(hid[:], part, -1.0, part, ALU.mult, ALU.max)
-            h_w = sb.tile([P, H], U32, name="h_w%d" % h, align_bytes=64)
-            h_s = sb.tile([P, H], U8, name="h_s%d" % h, align_bytes=64)
-            hid_ops.append((hid, h_w, h_s))
-        p_ps = [ps.tile([P, J], F32, name="p%d" % n, tag="a%d" % n) for n in range(N // P)]
+            for t in range(PACK):
+                movers[t // 2](read[h][t // 2][:, t % 2, :], boards[t][:].indirect(list4[:, list_halves[h]]))
+
+        diff = [sb.tile([P, PACK, HALF], F32, name="diff%d" % h) for h in range(2)]
         for h in range(2):
-            hid, h_w, h_s = hid_ops[h]
-            nc.vector.quantize_mx(out=h_w[:].bitcast(E5M2), scales=h_s[:], in_=hid[:].rearrange("p j t -> p (j t)"))
-            for n in range(N // P):
+            for g in range(2):
+                pair = slice(2 * g, 2 * g + 2)
+                nc.vector.tensor_tensor(diff[h][:, pair, :], read[h][g][:], b_acc[h][:, pair, :], ALU.subtract)
+
+        hid = [sb.tile([P, HALF, PACK], BF16, name="hid%d" % h, align_bytes=64) for h in range(2)]
+        woven = [diff[h][:].rearrange("p t j -> p j t") for h in range(2)]
+        nc.scalar.activation(hid[0][:], woven[0], ACT.Abs)
+        nc.scalar.activation(hid[1][:, 0:SHARE, :], woven[1][:, 0:SHARE, :], ACT.Abs)
+        rest = woven[1][:, SHARE:HALF, :]
+        nc.vector.scalar_tensor_tensor(hid[1][:, SHARE:HALF, :], rest, -1.0, rest, ALU.mult, ALU.max)
+
+        p_sb = [sb.tile([P, J], F32, name="p_sb%d" % n) for n in range(2)]
+        for h in range(2):
+            hid_codes = sb.tile([P, HALF], U32, name="hid_codes%d" % h, align_bytes=64)
+            hid_sc = sb.tile([P, HALF], U8, name="hid_sc%d" % h, align_bytes=64)
+            nc.vector.quantize_mx(
+                out=hid_codes[:].bitcast(E5M2), scales=hid_sc[:], in_=hid[h][:].rearrange("p j t -> p (j t)")
+            )
+            for n in range(2):
                 cols = slice(n * P, (n + 1) * P)
-                product(p_ps[n][:, halves[h]], (wb_w[:, cols].bitcast(E4M3), wb_s[:, cols]), (h_w[:].bitcast(E5M2), h_s[:]), True, True)
+                acc = ps.tile([P, HALF], F32, name="p%d_%d" % (h, n), tag="bank%d" % (2 * h + n))
+                wb_op = (wb_codes[:, cols].bitcast(E4M3), wb_plane[:, cols])
+                product(acc[:], wb_op, (hid_codes[:].bitcast(E5M2), hid_sc[:]), True, True)
+                (scalar_move if h == 0 else movers[n])(p_sb[n][:, halves[h]], acc[:])
 
-        copies = [v_copy, s_copy]
+        pairs = []
+        for n in range(2):
+            first = sb.tile([P, E], F32, name="first%d" % n)
+            second = sb.tile([P, E], F32, name="second%d" % n)
+            movers[n](first[:], p_sb[n][:].indirect(list5[:]))
+            movers[n](second[:], p_sb[n][:].indirect(list6[:]))
+            pairs.append((first, second))
+
         queues = [nc.sync, nc.scalar]
-        picked = []
-        for h in range(N // P):
-            acc = p_ps[h]
-            p_sb = sb.tile([P, J], F32, name="p_sb%d" % h)
-            copies[h](p_sb[:], acc[:])
-            one = sb.tile([P, E], F32, name="one%d" % h)
-            two = sb.tile([P, E], F32, name="two%d" % h)
-            copies[h](one[:], p_sb[:].indirect(o5[:]))
-            copies[h](two[:], p_sb[:].indirect(o6[:]))
-            picked.append((one, two))
-        for h in range(N // P):
-            best = sb.tile([P, E], F32, name="best%d" % h)
-            nc.vector.tensor_tensor(best[:], picked[h][0][:], picked[h][1][:], ALU.max)
-            queues[h].dma_start(out[h * P : (h + 1) * P, :], best[:])
+        for n in (1, 0):
+            best = sb.tile([P, E], F32, name="best%d" % n)
+            nc.vector.tensor_tensor(best[:], pairs[n][0][:], pairs[n][1][:], ALU.max)
+            queues[n].dma_start(out[n * P : (n + 1) * P, :], best[:])

@@ -21,6 +21,7 @@ P = 128
 PACK = 4
 QUADRANTS = 4
 LIST_ROWS = 16
+RUN = 4
 HALF = J // 2
 SHARE = HALF // 2
 
@@ -58,18 +59,18 @@ def tile_list_crossed_board_one_bestoftwo_kernel(
         def flat(words):
             return words[0].rearrange("p n t -> p (n t)")
 
-        xt_plane = zeroed_plane(T, "xt_plane")
         w_plane = zeroed_plane(R, "w_plane")
+        xt_plane = zeroed_plane(T, "xt_plane")
         xo_plane = zeroed_plane(Z, "xo_plane")
         w2_plane = zeroed_plane(R, "w2_plane")
         wb_plane = zeroed_plane(N, "wb_plane")
 
         list1 = load_list(offs, "list1")
         list2 = load_list(offs2, "list2")
-        load_scales(xt_plane, xt_scales, range(QUADRANTS))
+        load_scales(w_plane, w_scales, range(QUADRANTS))
         xt_tab = load_words(xt_words[0], U16, T, "xt_tab")
         xo_tab = load_words(flat(xo_words), U32, Z, "xo_tab")
-        load_scales(w_plane, w_scales, range(QUADRANTS))
+        load_scales(xt_plane, xt_scales, range(QUADRANTS))
         load_scales(xo_plane, xo_scales, range(1))
         w_raw = load_words(flat(w_words), U32, R, "w_raw")
         w2_raw = load_words(flat(w2_words), U32, R, "w2_raw")
@@ -93,22 +94,30 @@ def tile_list_crossed_board_one_bestoftwo_kernel(
             nc.vector.tensor_copy(picked[:], window[:].indirect(lst[:]))
             return picked
 
-        def deal(src, dtype, name, copy, parts):
-            dealt = sb.tile([P, PACK, P], dtype, name=name, align_bytes=64)
-            by_slice = src[:].rearrange("p (m t) -> p t m", t=PACK)
-            step = PACK // parts
-            for t in range(0, PACK, step):
-                copy(dealt[:, t : t + step, :], by_slice[:, t : t + step, :])
+        def deal_words(raw, name):
+            dealt = sb.tile([P, PACK, P], U32, name=name, align_bytes=64)
+            nc.scalar.copy(
+                dealt[:].rearrange("p t (c i) -> p c t i", i=RUN),
+                raw[:].rearrange("p (c i t) -> p c t i", i=RUN, t=PACK),
+            )
             return dealt
 
-        xt_sc = gather_packed(xt_plane, list1, U8, "xt_sc")
+        def deal_scales(plane, name, parts):
+            dealt = sb.tile([P, PACK, P], U8, name=name, align_bytes=64)
+            by_slice = plane[:].rearrange("p (m t) -> p t m", t=PACK)
+            step = PACK // parts
+            for t in range(0, PACK, step):
+                nc.vector.tensor_copy(dealt[:, t : t + step, :], by_slice[:, t : t + step, :])
+            return dealt
+
+        w_sc = deal_scales(w_plane, "w_sc", 1)
         xt_codes = gather_packed(xt_tab, list1, U16, "xt_codes")
         xo_codes = gather_packed(xo_tab, list2, U32, "xo_codes")
-        w_sc = deal(w_plane, U8, "w_sc", nc.vector.tensor_copy, 1)
-        w_codes = deal(w_raw, U32, "w_codes", nc.scalar.copy, 1)
-        w2_codes = deal(w2_raw, U32, "w2_codes", nc.scalar.copy, 1)
+        xt_sc = gather_packed(xt_plane, list1, U8, "xt_sc")
+        w_codes = deal_words(w_raw, "w_codes")
+        w2_codes = deal_words(w2_raw, "w2_codes")
         xo_sc = gather_packed(xo_plane, list2, U8, "xo_sc")
-        w2_sc = deal(w2_plane, U8, "w2_sc", nc.vector.tensor_copy, 2)
+        w2_sc = deal_scales(w2_plane, "w2_sc", 2)
 
         def xt_op(cols):
             return (xt_codes[:, cols].bitcast(E2M1), xt_sc[:, cols])
@@ -168,10 +177,17 @@ def tile_list_crossed_board_one_bestoftwo_kernel(
                 nc.vector.tensor_tensor(diff[h][:, pair, :], read[h][g][:], b_acc[h][:, pair, :], ALU.subtract)
 
         hid = [sb.tile([P, HALF, PACK], BF16, name="hid%d" % h, align_bytes=64) for h in range(2)]
-        woven = [diff[h][:].rearrange("p t j -> p j t") for h in range(2)]
-        nc.scalar.activation(hid[0][:], woven[0], ACT.Abs)
-        nc.scalar.activation(hid[1][:, 0:SHARE, :], woven[1][:, 0:SHARE, :], ACT.Abs)
-        rest = woven[1][:, SHARE:HALF, :]
+
+        def scalar_magnitude(h, slots):
+            nc.scalar.activation(
+                hid[h][:, slots, :].rearrange("p (c i) t -> p c t i", i=RUN),
+                diff[h][:, :, slots].rearrange("p t (c i) -> p c t i", i=RUN),
+                ACT.Abs,
+            )
+
+        scalar_magnitude(0, slice(0, HALF))
+        scalar_magnitude(1, slice(0, SHARE))
+        rest = diff[1][:, :, SHARE:HALF].rearrange("p t j -> p j t")
         nc.vector.scalar_tensor_tensor(hid[1][:, SHARE:HALF, :], rest, -1.0, rest, ALU.mult, ALU.max)
 
         p_sb = [sb.tile([P, J], F32, name="p_sb%d" % n) for n in range(2)]

from contextlib import ExitStack

import concourse.mybir as mybir

K, T, Z, J, R, C, N, E = 512, 1024, 1024, 256, 512, 512, 256, 128
FLOPS = 2 * (4 * K * R * J + R * N * J)

F32 = mybir.dt.float32
BF16 = mybir.dt.bfloat16
I32 = mybir.dt.int32
U32 = mybir.dt.uint32
U16 = mybir.dt.uint16
U8 = mybir.dt.uint8
E4M3 = mybir.dt.float8_e4m3fn_x4
E5M2 = mybir.dt.float8_e5m2_x4
E2M1 = mybir.dt.float4_e2m1fn_x4
ALU = mybir.AluOpType
ACT = mybir.ActivationFunctionType

P = 128
PACK = 4
QUADRANTS = 4
LIST_ROWS = 16
RUN = 4
HALF = J // 2
SHARE = HALF // 2


def tile_list_crossed_board_one_bestoftwo_kernel(
    tc, xt_words, xt_scales, xo_words, xo_scales, w_words, w_scales, w2_words, w2_scales,
    wb_words, wb_scales, offs, offs2, offs3, offs4, offs5, offs6, out,
):
    nc = tc.nc
    with ExitStack() as ctx:
        sb = ctx.enter_context(tc.tile_pool(name="sb", bufs=1))
        ps = ctx.enter_context(tc.psum_pool(name="ps", bufs=1))

        def load_list(src, name):
            lst = sb.tile(list(src.shape), U16, name=name)
            nc.sync.dma_start(lst[:], src)
            return lst

        def load_words(src, dtype, width, name):
            words = sb.tile([P, width], dtype, name=name, align_bytes=64)
            nc.sync.dma_start(words[:].bitcast(I32), src.bitcast(I32))
            return words

        def zeroed_plane(width, name):
            plane = sb.tile([P, width], U8, name=name, align_bytes=64)
            nc.vector.memset(plane[:].bitcast(I32), 0)
            return plane

        def load_scales(plane, src, quadrants):
            for q in quadrants:
                nc.sync.dma_start(
                    plane[32 * q : 32 * q + 4, :].bitcast(I32), src[0, 4 * q : 4 * q + 4, :].bitcast(I32)
                )

        def flat(words):
            return words[0].rearrange("p n t -> p (n t)")

        w_plane = zeroed_plane(R, "w_plane")
        xt_plane = zeroed_plane(T, "xt_plane")
        xo_plane = zeroed_plane(Z, "xo_plane")
        w2_plane = zeroed_plane(R, "w2_plane")
        wb_plane = zeroed_plane(N, "wb_plane")

        list1 = load_list(offs, "list1")
        list2 = load_list(offs2, "list2")
        load_scales(w_plane, w_scales, range(QUADRANTS))
        xt_tab = load_words(xt_words[0], U16, T, "xt_tab")
        xo_tab = load_words(flat(xo_words), U32, Z, "xo_tab")
        load_scales(xt_plane, xt_scales, range(QUADRANTS))
        load_scales(xo_plane, xo_scales, range(1))
        w_raw = load_words(flat(w_words), U32, R, "w_raw")
        w2_raw = load_words(flat(w2_words), U32, R, "w2_raw")
        load_scales(xo_plane, xo_scales, range(1, QUADRANTS))
        load_scales(w2_plane, w2_scales, range(QUADRANTS))
        list3 = load_list(offs3, "list3")
        list4 = load_list(offs4, "list4")
        wb_codes = load_words(flat(wb_words), U32, N, "wb_codes")
        load_scales(wb_plane, wb_scales, range(QUADRANTS))
        list5 = load_list(offs5, "list5")
        list6 = load_list(offs6, "list6")

        boards = []
        for t in range(PACK):
            board = sb.tile([P, C], F32, name="board%d" % t)
            nc.vector.memset(board[:], 0.0)
            boards.append(board)

        def gather_packed(window, lst, dtype, name):
            picked = sb.tile([P, J], dtype, name=name, align_bytes=64)
            nc.vector.tensor_copy(picked[:], window[:].indirect(lst[:]))
            return picked

        def deal_words(raw, name):
            dealt = sb.tile([P, PACK, P], U32, name=name, align_bytes=64)
            nc.scalar.copy(
                dealt[:].rearrange("p t (c i) -> p c t i", i=RUN),
                raw[:].rearrange("p (c i t) -> p c t i", i=RUN, t=PACK),
            )
            return dealt

        def deal_scales(plane, name, parts):
            dealt = sb.tile([P, PACK, P], U8, name=name, align_bytes=64)
            by_slice = plane[:].rearrange("p (m t) -> p t m", t=PACK)
            step = PACK // parts
            for t in range(0, PACK, step):
                nc.vector.tensor_copy(dealt[:, t : t + step, :], by_slice[:, t : t + step, :])
            return dealt

        w_sc = deal_scales(w_plane, "w_sc", 1)
        xt_codes = gather_packed(xt_tab, list1, U16, "xt_codes")
        xo_codes = gather_packed(xo_tab, list2, U32, "xo_codes")
        xt_sc = gather_packed(xt_plane, list1, U8, "xt_sc")
        w_codes = deal_words(w_raw, "w_codes")
        w2_codes = deal_words(w2_raw, "w2_codes")
        xo_sc = gather_packed(xo_plane, list2, U8, "xo_sc")
        w2_sc = deal_scales(w2_plane, "w2_sc", 2)

        def xt_op(cols):
            return (xt_codes[:, cols].bitcast(E2M1), xt_sc[:, cols])

        def xo_op(cols):
            return (xo_codes[:, cols].bitcast(E5M2), xo_sc[:, cols])

        def w_op(t):
            return (w_codes[:, t, :].bitcast(E5M2), w_sc[:, t, :])

        def w2_op(t):
            return (w2_codes[:, t, :].bitcast(E4M3), w2_sc[:, t, :])

        def product(acc, lhs, rhs, start, stop):
            nc.tensor.matmul_mx(
                out=acc, lhsT=lhs[0], lhsT_scale=lhs[1], rhs=rhs[0], rhs_scale=rhs[1], start=start, stop=stop
            )

        all_slots = slice(0, J)
        halves = [slice(0, HALF), slice(HALF, J)]
        list_halves = [slice(0, HALF // LIST_ROWS), slice(HALF // LIST_ROWS, J // LIST_ROWS)]

        a_acc = []
        for t in range(PACK):
            acc = ps.tile([P, J], F32, name="a%d" % t, tag="bank%d" % t)
            product(acc[:], w_op(t), xt_op(all_slots), True, False)
            product(acc[:], w2_op(t), xo_op(all_slots), False, True)
            a_acc.append(acc)
        b_acc = []
        for h in range(2):
            acc = ps.tile([P, PACK, HALF], F32, name="b%d" % h)
            for t in range(PACK):
                product(acc[:, t, :], w2_op(t), xt_op(halves[h]), True, False)
                product(acc[:, t, :], w_op(t), xo_op(halves[h]), False, True)
            b_acc.append(acc)

        def scalar_move(dst, src):
            nc.scalar.activation(dst, src, ACT.Copy)

        movers = [nc.vector.tensor_copy, scalar_move]

        a_sb = [sb.tile([P, J], F32, name="a_sb%d" % t) for t in range(PACK)]
        for t in range(PACK):
            movers[t // 2](a_sb[t][:], a_acc[t][:])
        for t in range(PACK):
            movers[t // 2](boards[t][:].indirect(list3[:]), a_sb[t][:])

        read = [[sb.tile([P, 2, HALF], F32, name="read%d_%d" % (h, g)) for g in range(2)] for h in range(2)]
        for h in range(2):
            for t in range(PACK):
                movers[t // 2](read[h][t // 2][:, t % 2, :], boards[t][:].indirect(list4[:, list_halves[h]]))

        diff = [sb.tile([P, PACK, HALF], F32, name="diff%d" % h) for h in range(2)]
        for h in range(2):
            for g in range(2):
                pair = slice(2 * g, 2 * g + 2)
                nc.vector.tensor_tensor(diff[h][:, pair, :], read[h][g][:], b_acc[h][:, pair, :], ALU.subtract)

        hid = [sb.tile([P, HALF, PACK], BF16, name="hid%d" % h, align_bytes=64) for h in range(2)]

        def scalar_magnitude(h, slots):
            nc.scalar.activation(
                hid[h][:, slots, :].rearrange("p (c i) t -> p c t i", i=RUN),
                diff[h][:, :, slots].rearrange("p t (c i) -> p c t i", i=RUN),
                ACT.Abs,
            )

        scalar_magnitude(0, slice(0, HALF))
        scalar_magnitude(1, slice(0, SHARE))
        rest = diff[1][:, :, SHARE:HALF].rearrange("p t j -> p j t")
        nc.vector.scalar_tensor_tensor(hid[1][:, SHARE:HALF, :], rest, -1.0, rest, ALU.mult, ALU.max)

        p_sb = [sb.tile([P, J], F32, name="p_sb%d" % n) for n in range(2)]
        for h in range(2):
            hid_codes = sb.tile([P, HALF], U32, name="hid_codes%d" % h, align_bytes=64)
            hid_sc = sb.tile([P, HALF], U8, name="hid_sc%d" % h, align_bytes=64)
            nc.vector.quantize_mx(
                out=hid_codes[:].bitcast(E5M2), scales=hid_sc[:], in_=hid[h][:].rearrange("p j t -> p (j t)")
            )
            for n in range(2):
                cols = slice(n * P, (n + 1) * P)
                acc = ps.tile([P, HALF], F32, name="p%d_%d" % (h, n), tag="bank%d" % (2 * h + n))
                wb_op = (wb_codes[:, cols].bitcast(E4M3), wb_plane[:, cols])
                product(acc[:], wb_op, (hid_codes[:].bitcast(E5M2), hid_sc[:]), True, True)
                (scalar_move if h == 0 else movers[n])(p_sb[n][:, halves[h]], acc[:])

        pairs = []
        for n in range(2):
            first = sb.tile([P, E], F32, name="first%d" % n)
            second = sb.tile([P, E], F32, name="second%d" % n)
            movers[n](first[:], p_sb[n][:].indirect(list5[:]))
            movers[n](second[:], p_sb[n][:].indirect(list6[:]))
            pairs.append((first, second))

        queues = [nc.sync, nc.scalar]
        for n in (1, 0):
            best = sb.tile([P, E], F32, name="best%d" % n)
            nc.vector.tensor_tensor(best[:], pairs[n][0][:], pairs[n][1][:], ALU.max)
            queues[n].dma_start(out[n * P : (n + 1) * P, :], best[:])
